import numpy as np
import ml_dtypes


def mxq(x, axis, fmt="e4m3"):
    dtype, down = {"e4m3": (ml_dtypes.float8_e4m3fn, 7), "e5m2": (ml_dtypes.float8_e5m2, 14)}[fmt]
    v = np.moveaxis(np.asarray(x, np.float32).astype(ml_dtypes.bfloat16).astype(np.float64), axis, -1)
    blocks = v.reshape(v.shape[:-1] + (-1, 32))
    amax = np.abs(blocks).max(-1, keepdims=True)
    byte = np.maximum(np.where(amax > 0, np.frexp(amax)[1] - 1 + 127, 0) - down, 1)
    scale = np.exp2(byte - 127.0)
    codes = (blocks / scale).astype(np.float32).astype(dtype).astype(np.float64)
    return np.moveaxis((codes * scale).reshape(v.shape), -1, axis)


WIDE = False


def mx_kscale(k):
    if not WIDE:
        return np.ones(k)
    levels = np.array([10, -10, 5, -5, 0])
    if k % 512:
        return np.exp2(np.random.permutation(np.resize(levels, k // 32))).repeat(32)
    a = np.empty((k // 512, 16))
    for p in range(k // 512):
        a[p, :8] = np.random.permutation(np.resize(levels, 8))
        for g in range(8):
            far = levels[np.abs(levels - a[p, g]) >= 10]
            a[p, g + 8] = far[np.random.randint(len(far))]
    return np.exp2(a.ravel()).repeat(32)


def f64(x):
    return np.asarray(x).astype(np.float64)


def striped(idx):
    return np.tile(idx.reshape(-1, 16).T, (8, 1)).astype(np.uint16)


def unstriped(offs):
    return offs[:16].T.reshape(-1).astype(np.int64)


def pack_weight(w):
    k, n = w.shape
    w = f64(np.asarray(w, np.float32).astype(ml_dtypes.bfloat16)).reshape(k // 32, 32, n)
    amax = np.abs(w).max(1)
    byte = np.clip(np.where(amax > 0, np.frexp(amax)[1] - 1 + 127 - 7, 1), 1, 254)
    scaled = (w * np.exp2(127.0 - byte)[:, None, :]).reshape(k, n).astype(np.float32)
    words = np.ascontiguousarray(scaled.reshape(k // 512, 128, 4, n).transpose(0, 1, 3, 2)).astype(ml_dtypes.float8_e4m3fn).view(np.uint8)
    return words, np.ascontiguousarray(byte.astype(np.uint8).reshape(k // 512, 16, n))


def unpack_weight(words, scales):
    g, p, n, _ = words.shape
    vals = np.ascontiguousarray(words).view(ml_dtypes.float8_e4m3fn).astype(np.float64) * np.repeat(np.exp2(scales.astype(np.float64) - 127.0), 8, axis=1)[..., None]
    return vals.transpose(0, 1, 3, 2).reshape(g * 512, n)


def relu2(v):
    return np.maximum(v, 0.0) ** 2


K, T, E, C, N = 3072, 1024, 4, 256, 256


def by_expert(wq, xq):
    return np.concatenate([wq[e].T @ xq[:, e * C:(e + 1) * C] for e in range(E)], axis=1)


def setup_inputs():
    n = np.random.standard_normal
    s = mx_kscale(K)[:, None]
    packed = [pack_weight(m) for m in n((E, K, N)) / np.sqrt(K) / s[None]]
    return {
        "xT": (n((K, T)) * s).astype(np.float32),
        "w_words": np.stack([m[0] for m in packed]),
        "w_scales": np.stack([m[1] for m in packed]),
        "b": (0.3 * n((N, E))).astype(np.float32),
        "gate": np.tile(np.random.uniform(0.2, 1.0, E * C), (N, 1)).astype(np.float32),
        "offs": striped(np.random.permutation(T)[:E * C]),
    }


def reference(xT, w_words, w_scales, b, gate, offs):
    idx = unstriped(offs)
    xq = mxq(f64(xT)[:, idx], 0, "e4m3")
    w = np.stack([unpack_weight(w_words[e], w_scales[e]) for e in range(E)])
    y = by_expert(w, xq)
    y = relu2(y + np.repeat(f64(b), C, axis=1))
    out = np.zeros((N, T))
    out[:, idx] = f64(gate) * y
    return out

@@ -1,0 +1,141 @@
+from contextlib import ExitStack
+
+import concourse.mybir as mybir
+
+K, T, E, C, N = 3072, 1024, 4, 256, 256
+P = 128
+PASSES = K // 512
+FLOPS = 2 * K * N * E * C
+BYTES = 4 * K * T + E * K * N + E * K * N // 32 + 4 * N * E + 4 * E * C + 2 * P * (E * C // 16) + 4 * N * T
+
+F32 = mybir.dt.float32
+BF16 = mybir.dt.bfloat16
+I32 = mybir.dt.int32
+U32 = mybir.dt.uint32
+U16 = mybir.dt.uint16
+U8 = mybir.dt.uint8
+FP8X4 = mybir.dt.float8_e4m3fn_x4
+RELU = mybir.ActivationFunctionType.Relu
+SQUARE = mybir.ActivationFunctionType.Square
+MULT = mybir.AluOpType.mult
+
+H = 512
+MID = [[(0, 512, 512)], [(0, 512, 256)]]
+CHUNKS = [[[(0, 256, 256), (256, 512, 256)], [(0, 512, 384)]], MID, MID, MID, MID, [[(0, 512, 512)], [(0, 256, 256), (256, 512, 256)]]]
+
+
+def tile_routed_moe_kernel(tc, xT, w_words, w_scales, b, gate, offs, out):
+    nc = tc.nc
+    xv = xT.rearrange("(a p t) n -> a p t n", p=P, t=4)
+
+    with ExitStack() as ctx:
+        keep = ctx.enter_context(tc.tile_pool(name="keep", bufs=1))
+        rawp = ctx.enter_context(tc.tile_pool(name="rawp", bufs=8))
+        grpp = ctx.enter_context(tc.tile_pool(name="grpp", bufs=6))
+        psum = ctx.enter_context(tc.psum_pool(name="psum", bufs=1))
+
+        offsets = keep.tile([P, E * C // 16], U16, name="offsets")
+        nc.sync.dma_start(offsets[:], offs)
+
+        bias = keep.tile([P, 2, E], F32, name="bias")
+        nc.gpsimd.dma_start(out=bias[:], in_=b.rearrange("(h p) e -> p h e", p=P))
+
+        qs = []
+        for g in range(2):
+            plane = keep.tile([P, T], U8, name=f"qs{g}", align_bytes=64)
+            nc.vector.memset(plane[:].bitcast(I32), 0)
+            qs.append(plane)
+        wsc = keep.tile([P, E * PASSES, N], U8, name="wsc", align_bytes=64)
+        nc.vector.memset(wsc[:].bitcast(I32), 0)
+
+        gw = {}
+        gs = {}
+
+        def gather_bytes(g, s):
+            t = keep.tile([P, H], U8, name=f"gs{g}{s}", align_bytes=64)
+            nc.vector.tensor_copy(t[:], qs[g][:].indirect(offsets[:, s * (H // 16):(s + 1) * (H // 16)]))
+            gs[g, s] = t
+
+        def gather_words(a, s, words):
+            t = keep.tile([P, H], U32, name=f"gw{a}{s}", align_bytes=64)
+            nc.vector.tensor_copy(t[:], words[:].indirect(offsets[:, s * (H // 16):(s + 1) * (H // 16)]))
+            gw[a, s] = t
+
+        wv = w_scales.rearrange("e a q n -> q (e a) n")
+        wt = {}
+
+        def load_scales():
+            for q in range(4):
+                nc.sync.dma_start(out=wsc[32 * q:32 * q + 4].bitcast(I32), in_=wv[4 * q:4 * q + 4].bitcast(I32))
+
+        def load_w(e):
+            w = keep.tile([P, PASSES, N], U32, name=f"w{e}", align_bytes=64)
+            nc.sync.dma_start(out=w[:].bitcast(I32), in_=w_words[e].rearrange("a p n r -> p a (n r)").bitcast(I32))
+            wt[e] = w
+
+        for a in range(PASSES):
+            words = keep.tile([P, T], U32, name=f"qw{a}", align_bytes=64)
+            g, k = a // 4, 4 * (a % 4)
+            if a == 5:
+                load_scales()
+                load_w(0)
+            for s in range(2):
+                grouped = grpp.tile([P, H, 4], BF16, name="grouped", align_bytes=64)
+                for lo, hi, cut in CHUNKS[a][s]:
+                    raw = rawp.tile([P, 4, hi - lo], F32, name="raw", align_bytes=64)
+                    nc.sync.dma_start(out=raw[:], in_=xv[a, :, :, s * H + lo:s * H + hi])
+                    if cut > lo:
+                        nc.scalar.copy(grouped[:, lo:cut, :], raw[:, :, 0:cut - lo].rearrange("p t n -> p n t"))
+                    if cut < hi:
+                        nc.vector.tensor_copy(grouped[:, cut:hi, :], raw[:, :, cut - lo:hi - lo].rearrange("p t n -> p n t"))
+                nc.vector.quantize_mx(
+                    out=words[:, s * H:(s + 1) * H].bitcast(FP8X4),
+                    scales=qs[g][k:P, s * H:(s + 1) * H],
+                    in_=grouped[:].rearrange("p n t -> p (n t)"),
+                )
+            for s in range(2):
+                if a in (3, 5):
+                    gather_bytes(g, s)
+                gather_words(a, s, words)
+
+        load_w(1)
+        gate_sb = keep.tile([P, E * C], F32, name="gate_sb")
+        nc.sync.dma_start(out=gate_sb[:], in_=gate[0:P, :])
+        load_w(2)
+        load_w(3)
+
+        win = []
+        for h in range(2):
+            window = keep.tile([P, T], F32, name=f"win{h}")
+            win.append(window)
+        for s in range(2):
+            acc = {}
+            for e in (2 * s, 2 * s + 1):
+                for h in range(2):
+                    acc[e, h] = psum.tile([P, C], F32, name=f"acc{e}{h}")
+                for a in range(PASSES):
+                    g, k = a // 4, 4 * (a % 4)
+                    cols = slice((e % 2) * C, (e % 2 + 1) * C)
+                    for h in range(2):
+                        rows = slice(h * P, (h + 1) * P)
+                        nc.tensor.matmul_mx(
+                            out=acc[e, h][:],
+                            lhsT=wt[e][:, a, rows].bitcast(FP8X4),
+                            lhsT_scale=wsc[:, e * PASSES + a, rows],
+                            rhs=gw[a, s][:, cols].bitcast(FP8X4),
+                            rhs_scale=gs[g, s][k:P, cols],
+                            start=(a == 0),
+                            stop=(a == PASSES - 1),
+                        )
+            for h in range(2):
+                r = keep.tile([P, H], F32, name=f"r{s}{h}")
+                sq = keep.tile([P, H], F32, name=f"sq{s}{h}")
+                val = keep.tile([P, H], F32, name=f"val{s}{h}")
+                for i in range(2):
+                    e = 2 * s + i
+                    nc.scalar.activation(r[:, i * C:(i + 1) * C], acc[e, h][:], RELU, bias=bias[:, h, e:e + 1])
+                nc.scalar.activation(sq[:], r[:], SQUARE)
+                nc.vector.tensor_tensor(val[:], sq[:], gate_sb[:, s * H:(s + 1) * H], MULT)
+                nc.vector.tensor_copy(win[h][:].indirect(offsets[:, s * (H // 16):(s + 1) * (H // 16)]), val[:])
+        for h in range(2):
+            nc.sync.dma_start(out=out[h * P:(h + 1) * P, :], in_=win[h][:])

@@ -35,10 +35,8 @@ def tile_routed_moe_kernel(tc, xT, w_words, w_scales, b, gate, offs, out):
         psum = ctx.enter_context(tc.psum_pool(name="psum", bufs=1))
 
         offsets = keep.tile([P, E * C // 16], U16, name="offsets")
-        nc.sync.dma_start(offsets[:], offs)
-
         bias = keep.tile([P, 2, E], F32, name="bias")
-        nc.gpsimd.dma_start(out=bias[:], in_=b.rearrange("(h p) e -> p h e", p=P))
+        nc.scalar.dma_start(out=bias[:], in_=b.rearrange("(h p) e -> p h e", p=P))
 
         qs = []
         for g in range(2):
@@ -84,10 +82,12 @@ def tile_routed_moe_kernel(tc, xT, w_words, w_scales, b, gate, offs, out):
                 for lo, hi, cut in CHUNKS[a][s]:
                     raw = rawp.tile([P, 4, hi - lo], F32, name="raw", align_bytes=64)
                     nc.sync.dma_start(out=raw[:], in_=xv[a, :, :, s * H + lo:s * H + hi])
+                    if a == 0 and s == 0 and lo == 0:
+                        nc.sync.dma_start(offsets[:], offs)
                     if cut > lo:
-                        nc.scalar.copy(grouped[:, lo:cut, :], raw[:, :, 0:cut - lo].rearrange("p t n -> p n t"))
+                        nc.scalar.copy(grouped[:, lo:cut, :].rearrange("p (c i) t -> p c t i", i=4), raw[:, :, 0:cut - lo].rearrange("p t (c i) -> p c t i", i=4))
                     if cut < hi:
-                        nc.vector.tensor_copy(grouped[:, cut:hi, :], raw[:, :, cut - lo:hi - lo].rearrange("p t n -> p n t"))
+                        nc.vector.tensor_copy(grouped[:, cut:hi, :].rearrange("p (c i) t -> p c t i", i=4), raw[:, :, cut - lo:hi - lo].rearrange("p t (c i) -> p c t i", i=4))
                 nc.vector.quantize_mx(
                     out=words[:, s * H:(s + 1) * H].bitcast(FP8X4),
                     scales=qs[g][k:P, s * H:(s + 1) * H],
@@ -130,12 +130,10 @@ def tile_routed_moe_kernel(tc, xT, w_words, w_scales, b, gate, offs, out):
             for h in range(2):
                 r = keep.tile([P, H], F32, name=f"r{s}{h}")
                 sq = keep.tile([P, H], F32, name=f"sq{s}{h}")
-                val = keep.tile([P, H], F32, name=f"val{s}{h}")
                 for i in range(2):
                     e = 2 * s + i
                     nc.scalar.activation(r[:, i * C:(i + 1) * C], acc[e, h][:], RELU, bias=bias[:, h, e:e + 1])
                 nc.scalar.activation(sq[:], r[:], SQUARE)
-                nc.vector.tensor_tensor(val[:], sq[:], gate_sb[:, s * H:(s + 1) * H], MULT)
-                nc.vector.tensor_copy(win[h][:].indirect(offsets[:, s * (H // 16):(s + 1) * (H // 16)]), val[:])
+                nc.vector.tensor_tensor(win[h][:].indirect(offsets[:, s * (H // 16):(s + 1) * (H // 16)]), sq[:], gate_sb[:, s * H:(s + 1) * H], MULT)
         for h in range(2):
             nc.sync.dma_start(out=out[h * P:(h + 1) * P, :], in_=win[h][:])

@@ -20,8 +20,12 @@ SQUARE = mybir.ActivationFunctionType.Square
 MULT = mybir.AluOpType.mult
 
 H = 512
-MID = [[(0, 512, 512)], [(0, 512, 256)]]
-CHUNKS = [[[(0, 256, 256), (256, 512, 256)], [(0, 512, 384)]], MID, MID, MID, MID, [[(0, 512, 512)], [(0, 256, 256), (256, 512, 256)]]]
+WHOLE = [(0, 1024)]
+LOADS = [[(0, 256), (256, 512), (512, 1024)], WHOLE, WHOLE, WHOLE, WHOLE, [(0, 512), (512, 768), (768, 1024)]]
+MIDS = [[(0, 512)], [(512, 896)]]
+MIDV = [[], [(896, 1024)]]
+SCALAR_PART = [[[(0, 256)], [(512, 768)]], MIDS, MIDS, MIDS, MIDS, [[(0, 512)], [(512, 768)]]]
+VECTOR_PART = [[[(256, 512)], [(768, 1024)]], MIDV, MIDV, MIDV, MIDV, [[], [(768, 1024)]]]
 
 
 def tile_routed_moe_kernel(tc, xT, w_words, w_scales, b, gate, offs, out):
@@ -30,8 +34,8 @@ def tile_routed_moe_kernel(tc, xT, w_words, w_scales, b, gate, offs, out):
 
     with ExitStack() as ctx:
         keep = ctx.enter_context(tc.tile_pool(name="keep", bufs=1))
-        rawp = ctx.enter_context(tc.tile_pool(name="rawp", bufs=8))
-        grpp = ctx.enter_context(tc.tile_pool(name="grpp", bufs=6))
+        rawp = ctx.enter_context(tc.tile_pool(name="rawp", bufs=4))
+        grpp = ctx.enter_context(tc.tile_pool(name="grpp", bufs=4))
         psum = ctx.enter_context(tc.psum_pool(name="psum", bufs=1))
 
         offsets = keep.tile([P, E * C // 16], U16, name="offsets")
@@ -71,32 +75,51 @@ def tile_routed_moe_kernel(tc, xT, w_words, w_scales, b, gate, offs, out):
             nc.sync.dma_start(out=w[:].bitcast(I32), in_=w_words[e].rearrange("a p n r -> p a (n r)").bitcast(I32))
             wt[e] = w
 
+        def find(pieces, lo, hi):
+            for plo, phi, tile in pieces:
+                if plo <= lo and hi <= phi:
+                    return tile[:, :, lo - plo:hi - plo]
+
+        allwords = []
         for a in range(PASSES):
             words = keep.tile([P, T], U32, name=f"qw{a}", align_bytes=64)
+            allwords.append(words)
             g, k = a // 4, 4 * (a % 4)
             if a == 5:
                 load_scales()
                 load_w(0)
+            pieces = []
+            for lo, hi in LOADS[a]:
+                raw = rawp.tile([P, 4, hi - lo], F32, name=f"raw{hi - lo}", bufs=4 if hi - lo != 512 else 2, align_bytes=64)
+                nc.sync.dma_start(out=raw[:], in_=xv[a, :, :, lo:hi])
+                pieces.append((lo, hi, raw))
+                if a == 0 and lo == 0:
+                    nc.sync.dma_start(offsets[:], offs)
+            halves = []
             for s in range(2):
                 grouped = grpp.tile([P, H, 4], BF16, name="grouped", align_bytes=64)
-                for lo, hi, cut in CHUNKS[a][s]:
-                    raw = rawp.tile([P, 4, hi - lo], F32, name="raw", align_bytes=64)
-                    nc.sync.dma_start(out=raw[:], in_=xv[a, :, :, s * H + lo:s * H + hi])
-                    if a == 0 and s == 0 and lo == 0:
-                        nc.sync.dma_start(offsets[:], offs)
-                    if cut > lo:
-                        nc.scalar.copy(grouped[:, lo:cut, :].rearrange("p (c i) t -> p c t i", i=4), raw[:, :, 0:cut - lo].rearrange("p t (c i) -> p c t i", i=4))
-                    if cut < hi:
-                        nc.vector.tensor_copy(grouped[:, cut:hi, :].rearrange("p (c i) t -> p c t i", i=4), raw[:, :, cut - lo:hi - lo].rearrange("p t (c i) -> p c t i", i=4))
+                halves.append(grouped)
+                for engine, parts in ((nc.scalar.copy, SCALAR_PART[a][s]), (nc.vector.tensor_copy, VECTOR_PART[a][s])):
+                    for lo, hi in parts:
+                        engine(
+                            grouped[:, lo - s * H:hi - s * H, :].rearrange("p (c i) t -> p c t i", i=4),
+                            find(pieces, lo, hi).rearrange("p t (c i) -> p c t i", i=4),
+                        )
+            if a > 0:
+                for s in range(2):
+                    gather_words(a - 1, s, allwords[a - 1])
+            if a == 4:
+                for s in range(2):
+                    gather_bytes(0, s)
+            for s in range(2):
                 nc.vector.quantize_mx(
                     out=words[:, s * H:(s + 1) * H].bitcast(FP8X4),
                     scales=qs[g][k:P, s * H:(s + 1) * H],
-                    in_=grouped[:].rearrange("p n t -> p (n t)"),
+                    in_=halves[s][:].rearrange("p n t -> p (n t)"),
                 )
-            for s in range(2):
-                if a in (3, 5):
-                    gather_bytes(g, s)
-                gather_words(a, s, words)
+        for s in range(2):
+            gather_bytes(1, s)
+            gather_words(5, s, allwords[5])
 
         load_w(1)
         gate_sb = keep.tile([P, E * C], F32, name="gate_sb")
@@ -108,32 +131,30 @@ def tile_routed_moe_kernel(tc, xT, w_words, w_scales, b, gate, offs, out):
         for h in range(2):
             window = keep.tile([P, T], F32, name=f"win{h}")
             win.append(window)
-        for s in range(2):
-            acc = {}
-            for e in (2 * s, 2 * s + 1):
-                for h in range(2):
-                    acc[e, h] = psum.tile([P, C], F32, name=f"acc{e}{h}")
-                for a in range(PASSES):
-                    g, k = a // 4, 4 * (a % 4)
-                    cols = slice((e % 2) * C, (e % 2 + 1) * C)
-                    for h in range(2):
-                        rows = slice(h * P, (h + 1) * P)
-                        nc.tensor.matmul_mx(
-                            out=acc[e, h][:],
-                            lhsT=wt[e][:, a, rows].bitcast(FP8X4),
-                            lhsT_scale=wsc[:, e * PASSES + a, rows],
-                            rhs=gw[a, s][:, cols].bitcast(FP8X4),
-                            rhs_scale=gs[g, s][k:P, cols],
-                            start=(a == 0),
-                            stop=(a == PASSES - 1),
-                        )
+        for e in range(E):
+            s, cols, slots = e // 2, slice((e % 2) * C, (e % 2 + 1) * C), slice(e * C, (e + 1) * C)
+            acc = []
             for h in range(2):
-                r = keep.tile([P, H], F32, name=f"r{s}{h}")
-                sq = keep.tile([P, H], F32, name=f"sq{s}{h}")
-                for i in range(2):
-                    e = 2 * s + i
-                    nc.scalar.activation(r[:, i * C:(i + 1) * C], acc[e, h][:], RELU, bias=bias[:, h, e:e + 1])
+                bank = psum.tile([P, C], F32, name=f"acc{e}{h}")
+                acc.append(bank)
+            for a in range(PASSES):
+                g, k = a // 4, 4 * (a % 4)
+                for h in range(2):
+                    rows = slice(h * P, (h + 1) * P)
+                    nc.tensor.matmul_mx(
+                        out=acc[h][:],
+                        lhsT=wt[e][:, a, rows].bitcast(FP8X4),
+                        lhsT_scale=wsc[:, e * PASSES + a, rows],
+                        rhs=gw[a, s][:, cols].bitcast(FP8X4),
+                        rhs_scale=gs[g, s][k:P, cols],
+                        start=(a == 0),
+                        stop=(a == PASSES - 1),
+                    )
+            for h in range(2):
+                r = keep.tile([P, C], F32, name=f"r{e}{h}")
+                sq = keep.tile([P, C], F32, name=f"sq{e}{h}")
+                nc.scalar.activation(r[:], acc[h][:], RELU, bias=bias[:, h, e:e + 1])
                 nc.scalar.activation(sq[:], r[:], SQUARE)
-                nc.vector.tensor_tensor(win[h][:].indirect(offsets[:, s * (H // 16):(s + 1) * (H // 16)]), sq[:], gate_sb[:, s * H:(s + 1) * H], MULT)
+                nc.vector.tensor_tensor(win[h][:].indirect(offsets[:, e * (C // 16):(e + 1) * (C // 16)]), sq[:], gate_sb[:, slots], MULT)
         for h in range(2):
             nc.sync.dma_start(out=out[h * P:(h + 1) * P, :], in_=win[h][:])

@@ -105,18 +105,16 @@ def tile_routed_moe_kernel(tc, xT, w_words, w_scales, b, gate, offs, out):
                             grouped[:, lo - s * H:hi - s * H, :].rearrange("p (c i) t -> p c t i", i=4),
                             find(pieces, lo, hi).rearrange("p t (c i) -> p c t i", i=4),
                         )
-            if a > 0:
-                for s in range(2):
-                    gather_words(a - 1, s, allwords[a - 1])
-            if a == 4:
-                for s in range(2):
-                    gather_bytes(0, s)
             for s in range(2):
                 nc.vector.quantize_mx(
                     out=words[:, s * H:(s + 1) * H].bitcast(FP8X4),
                     scales=qs[g][k:P, s * H:(s + 1) * H],
                     in_=halves[s][:].rearrange("p n t -> p (n t)"),
                 )
+                if a > 0:
+                    gather_words(a - 1, s, allwords[a - 1])
+                if a == 4:
+                    gather_bytes(0, s)
         for s in range(2):
             gather_bytes(1, s)
             gather_words(5, s, allwords[5])
@@ -155,6 +153,8 @@ def tile_routed_moe_kernel(tc, xT, w_words, w_scales, b, gate, offs, out):
                 sq = keep.tile([P, C], F32, name=f"sq{e}{h}")
                 nc.scalar.activation(r[:], acc[h][:], RELU, bias=bias[:, h, e:e + 1])
                 nc.scalar.activation(sq[:], r[:], SQUARE)
-                nc.vector.tensor_tensor(win[h][:].indirect(offsets[:, e * (C // 16):(e + 1) * (C // 16)]), sq[:], gate_sb[:, slots], MULT)
+                val = keep.tile([P, C], F32, name=f"val{e}{h}")
+                nc.gpsimd.tensor_tensor(val[:], sq[:], gate_sb[:, slots], MULT)
+                nc.vector.tensor_copy(win[h][:].indirect(offsets[:, e * (C // 16):(e + 1) * (C // 16)]), val[:])
         for h in range(2):
             nc.sync.dma_start(out=out[h * P:(h + 1) * P, :], in_=win[h][:])

@@ -21,11 +21,15 @@ MULT = mybir.AluOpType.mult
 
 H = 512
 WHOLE = [(0, 1024)]
-LOADS = [[(0, 256), (256, 512), (512, 1024)], WHOLE, WHOLE, WHOLE, WHOLE, [(0, 512), (512, 768), (768, 1024)]]
-MIDS = [[(0, 512)], [(512, 896)]]
-MIDV = [[], [(896, 1024)]]
-SCALAR_PART = [[[(0, 256)], [(512, 768)]], MIDS, MIDS, MIDS, MIDS, [[(0, 512)], [(512, 768)]]]
-VECTOR_PART = [[[(256, 512)], [(768, 1024)]], MIDV, MIDV, MIDV, MIDV, [[], [(768, 1024)]]]
+WHOLE = [(0, 1024)]
+WHOLE = [(0, 1024)]
+HALVES = [(0, 512), (512, 1024)]
+LOADS = [[(0, 256), (256, 512), (512, 1024)], HALVES, WHOLE, WHOLE, WHOLE, [(0, 512), (512, 768), (768, 1024)]]
+MIDS = [[(0, 512)], [(512, 928)]]
+MIDV = [[], [(928, 1024)]]
+SCALAR_PART = [[[(0, 256)], [(512, 704)]], [[(0, 512)], [(512, 832)]], MIDS, MIDS, MIDS, [[(0, 512)], [(512, 768), (768, 864)]]]
+VECTOR_PART = [[[(256, 512)], [(704, 1024)]], [[], [(832, 1024)]], MIDV, MIDV, MIDV, [[], [(864, 1024)]]]
+QUANT = [512, 512, 512, 512, 512, 256]
 
 
 def tile_routed_moe_kernel(tc, xT, w_words, w_scales, b, gate, offs, out):
@@ -80,17 +84,14 @@ def tile_routed_moe_kernel(tc, xT, w_words, w_scales, b, gate, offs, out):
                 if plo <= lo and hi <= phi:
                     return tile[:, :, lo - plo:hi - plo]
 
-        allwords = []
         for a in range(PASSES):
             words = keep.tile([P, T], U32, name=f"qw{a}", align_bytes=64)
-            allwords.append(words)
             g, k = a // 4, 4 * (a % 4)
             if a == 5:
                 load_scales()
-                load_w(0)
             pieces = []
             for lo, hi in LOADS[a]:
-                raw = rawp.tile([P, 4, hi - lo], F32, name=f"raw{hi - lo}", bufs=4 if hi - lo != 512 else 2, align_bytes=64)
+                raw = rawp.tile([P, 4, hi - lo], F32, name=f"raw{hi - lo}", bufs={1024: 3, 512: 4, 256: 4}[hi - lo], align_bytes=64)
                 nc.sync.dma_start(out=raw[:], in_=xv[a, :, :, lo:hi])
                 pieces.append((lo, hi, raw))
                 if a == 0 and lo == 0:
@@ -106,19 +107,19 @@ def tile_routed_moe_kernel(tc, xT, w_words, w_scales, b, gate, offs, out):
                             find(pieces, lo, hi).rearrange("p t (c i) -> p c t i", i=4),
                         )
             for s in range(2):
-                nc.vector.quantize_mx(
-                    out=words[:, s * H:(s + 1) * H].bitcast(FP8X4),
-                    scales=qs[g][k:P, s * H:(s + 1) * H],
-                    in_=halves[s][:].rearrange("p n t -> p (n t)"),
-                )
-                if a > 0:
-                    gather_words(a - 1, s, allwords[a - 1])
-                if a == 4:
-                    gather_bytes(0, s)
-        for s in range(2):
-            gather_bytes(1, s)
-            gather_words(5, s, allwords[5])
+                for lo in range(0, H, QUANT[a]):
+                    cols = slice(s * H + lo, s * H + lo + QUANT[a])
+                    nc.vector.quantize_mx(
+                        out=words[:, cols].bitcast(FP8X4),
+                        scales=qs[g][k:P, cols],
+                        in_=halves[s][:, lo:lo + QUANT[a], :].rearrange("p n t -> p (n t)"),
+                    )
+            for s in range(2):
+                if a in (3, 5):
+                    gather_bytes(g, s)
+                gather_words(a, s, words)
 
+        load_w(0)
         load_w(1)
         gate_sb = keep.tile([P, E * C], F32, name="gate_sb")
         nc.sync.dma_start(out=gate_sb[:], in_=gate[0:P, :])
@@ -153,8 +154,6 @@ def tile_routed_moe_kernel(tc, xT, w_words, w_scales, b, gate, offs, out):
                 sq = keep.tile([P, C], F32, name=f"sq{e}{h}")
                 nc.scalar.activation(r[:], acc[h][:], RELU, bias=bias[:, h, e:e + 1])
                 nc.scalar.activation(sq[:], r[:], SQUARE)
-                val = keep.tile([P, C], F32, name=f"val{e}{h}")
-                nc.gpsimd.tensor_tensor(val[:], sq[:], gate_sb[:, slots], MULT)
-                nc.vector.tensor_copy(win[h][:].indirect(offsets[:, e * (C // 16):(e + 1) * (C // 16)]), val[:])
+                nc.vector.tensor_tensor(win[h][:].indirect(offsets[:, e * (C // 16):(e + 1) * (C // 16)]), sq[:], gate_sb[:, slots], MULT)
         for h in range(2):
             nc.sync.dma_start(out=out[h * P:(h + 1) * P, :], in_=win[h][:])

from contextlib import ExitStack

import concourse.mybir as mybir

K, T, E, C, N = 3072, 1024, 4, 256, 256
P = 128
PASSES = K // 512
FLOPS = 2 * K * N * E * C
BYTES = 4 * K * T + E * K * N + E * K * N // 32 + 4 * N * E + 4 * E * C + 2 * P * (E * C // 16) + 4 * N * T

F32 = mybir.dt.float32
BF16 = mybir.dt.bfloat16
I32 = mybir.dt.int32
U32 = mybir.dt.uint32
U16 = mybir.dt.uint16
U8 = mybir.dt.uint8
FP8X4 = mybir.dt.float8_e4m3fn_x4
RELU = mybir.ActivationFunctionType.Relu
SQUARE = mybir.ActivationFunctionType.Square
MULT = mybir.AluOpType.mult

H = 512
WHOLE = [(0, 1024)]
WHOLE = [(0, 1024)]
WHOLE = [(0, 1024)]
HALVES = [(0, 512), (512, 1024)]
LOADS = [[(0, 256), (256, 512), (512, 1024)], HALVES, WHOLE, WHOLE, WHOLE, [(0, 512), (512, 768), (768, 1024)]]
MIDS = [[(0, 512)], [(512, 928)]]
MIDV = [[], [(928, 1024)]]
SCALAR_PART = [[[(0, 256)], [(512, 704)]], [[(0, 512)], [(512, 832)]], MIDS, MIDS, MIDS, [[(0, 512)], [(512, 768), (768, 864)]]]
VECTOR_PART = [[[(256, 512)], [(704, 1024)]], [[], [(832, 1024)]], MIDV, MIDV, MIDV, [[], [(864, 1024)]]]
QUANT = [512, 512, 512, 512, 512, 256]


def tile_routed_moe_kernel(tc, xT, w_words, w_scales, b, gate, offs, out):
    nc = tc.nc
    xv = xT.rearrange("(a p t) n -> a p t n", p=P, t=4)

    with ExitStack() as ctx:
        keep = ctx.enter_context(tc.tile_pool(name="keep", bufs=1))
        rawp = ctx.enter_context(tc.tile_pool(name="rawp", bufs=4))
        grpp = ctx.enter_context(tc.tile_pool(name="grpp", bufs=4))
        psum = ctx.enter_context(tc.psum_pool(name="psum", bufs=1))

        offsets = keep.tile([P, E * C // 16], U16, name="offsets")
        bias = keep.tile([P, 2, E], F32, name="bias")
        nc.scalar.dma_start(out=bias[:], in_=b.rearrange("(h p) e -> p h e", p=P))

        qs = []
        for g in range(2):
            plane = keep.tile([P, T], U8, name=f"qs{g}", align_bytes=64)
            nc.vector.memset(plane[:].bitcast(I32), 0)
            qs.append(plane)
        wsc = keep.tile([P, E * PASSES, N], U8, name="wsc", align_bytes=64)
        nc.vector.memset(wsc[:].bitcast(I32), 0)

        gw = {}
        gs = {}

        def gather_bytes(g, s):
            t = keep.tile([P, H], U8, name=f"gs{g}{s}", align_bytes=64)
            nc.vector.tensor_copy(t[:], qs[g][:].indirect(offsets[:, s * (H // 16):(s + 1) * (H // 16)]))
            gs[g, s] = t

        def gather_words(a, s, words):
            t = keep.tile([P, H], U32, name=f"gw{a}{s}", align_bytes=64)
            nc.vector.tensor_copy(t[:], words[:].indirect(offsets[:, s * (H // 16):(s + 1) * (H // 16)]))
            gw[a, s] = t

        wv = w_scales.rearrange("e a q n -> q (e a) n")
        wt = {}

        def load_scales():
            for q in range(4):
                nc.sync.dma_start(out=wsc[32 * q:32 * q + 4].bitcast(I32), in_=wv[4 * q:4 * q + 4].bitcast(I32))

        def load_w(e):
            w = keep.tile([P, PASSES, N], U32, name=f"w{e}", align_bytes=64)
            nc.sync.dma_start(out=w[:].bitcast(I32), in_=w_words[e].rearrange("a p n r -> p a (n r)").bitcast(I32))
            wt[e] = w

        def find(pieces, lo, hi):
            for plo, phi, tile in pieces:
                if plo <= lo and hi <= phi:
                    return tile[:, :, lo - plo:hi - plo]

        for a in range(PASSES):
            words = keep.tile([P, T], U32, name=f"qw{a}", align_bytes=64)
            g, k = a // 4, 4 * (a % 4)
            if a == 5:
                load_scales()
            pieces = []
            for lo, hi in LOADS[a]:
                raw = rawp.tile([P, 4, hi - lo], F32, name=f"raw{hi - lo}", bufs={1024: 3, 512: 4, 256: 4}[hi - lo], align_bytes=64)
                nc.sync.dma_start(out=raw[:], in_=xv[a, :, :, lo:hi])
                pieces.append((lo, hi, raw))
                if a == 0 and lo == 0:
                    nc.sync.dma_start(offsets[:], offs)
            halves = []
            for s in range(2):
                grouped = grpp.tile([P, H, 4], BF16, name="grouped", align_bytes=64)
                halves.append(grouped)
                for engine, parts in ((nc.scalar.copy, SCALAR_PART[a][s]), (nc.vector.tensor_copy, VECTOR_PART[a][s])):
                    for lo, hi in parts:
                        engine(
                            grouped[:, lo - s * H:hi - s * H, :].rearrange("p (c i) t -> p c t i", i=4),
                            find(pieces, lo, hi).rearrange("p t (c i) -> p c t i", i=4),
                        )
            for s in range(2):
                for lo in range(0, H, QUANT[a]):
                    cols = slice(s * H + lo, s * H + lo + QUANT[a])
                    nc.vector.quantize_mx(
                        out=words[:, cols].bitcast(FP8X4),
                        scales=qs[g][k:P, cols],
                        in_=halves[s][:, lo:lo + QUANT[a], :].rearrange("p n t -> p (n t)"),
                    )
            for s in range(2):
                if a in (3, 5):
                    gather_bytes(g, s)
                gather_words(a, s, words)

        load_w(0)
        load_w(1)
        gate_sb = keep.tile([P, E * C], F32, name="gate_sb")
        nc.sync.dma_start(out=gate_sb[:], in_=gate[0:P, :])
        load_w(2)
        load_w(3)

        win = []
        for h in range(2):
            window = keep.tile([P, T], F32, name=f"win{h}")
            win.append(window)
        for e in range(E):
            s, cols, slots = e // 2, slice((e % 2) * C, (e % 2 + 1) * C), slice(e * C, (e + 1) * C)
            acc = []
            for h in range(2):
                bank = psum.tile([P, C], F32, name=f"acc{e}{h}")
                acc.append(bank)
            for a in range(PASSES):
                g, k = a // 4, 4 * (a % 4)
                for h in range(2):
                    rows = slice(h * P, (h + 1) * P)
                    nc.tensor.matmul_mx(
                        out=acc[h][:],
                        lhsT=wt[e][:, a, rows].bitcast(FP8X4),
                        lhsT_scale=wsc[:, e * PASSES + a, rows],
                        rhs=gw[a, s][:, cols].bitcast(FP8X4),
                        rhs_scale=gs[g, s][k:P, cols],
                        start=(a == 0),
                        stop=(a == PASSES - 1),
                    )
            for h in range(2):
                r = keep.tile([P, C], F32, name=f"r{e}{h}")
                sq = keep.tile([P, C], F32, name=f"sq{e}{h}")
                nc.scalar.activation(r[:], acc[h][:], RELU, bias=bias[:, h, e:e + 1])
                nc.scalar.activation(sq[:], r[:], SQUARE)
                nc.vector.tensor_tensor(win[h][:].indirect(offsets[:, e * (C // 16):(e + 1) * (C // 16)]), sq[:], gate_sb[:, slots], MULT)
        for h in range(2):
            nc.sync.dma_start(out=out[h * P:(h + 1) * P, :], in_=win[h][:])
